import numpy as np
import ml_dtypes


def mxq(x, axis, fmt="e4m3"):
    dtype, down = {"e4m3": (ml_dtypes.float8_e4m3fn, 7), "e5m2": (ml_dtypes.float8_e5m2, 14)}[fmt]
    v = np.moveaxis(np.asarray(x, np.float32).astype(ml_dtypes.bfloat16).astype(np.float64), axis, -1)
    blocks = v.reshape(v.shape[:-1] + (-1, 32))
    amax = np.abs(blocks).max(-1, keepdims=True)
    byte = np.maximum(np.where(amax > 0, np.frexp(amax)[1] - 1 + 127, 0) - down, 1)
    scale = np.exp2(byte - 127.0)
    codes = (blocks / scale).astype(np.float32).astype(dtype).astype(np.float64)
    return np.moveaxis((codes * scale).reshape(v.shape), -1, axis)


WIDE = False


def mx_kscale(k):
    if not WIDE:
        return np.ones(k)
    levels = np.array([10, -10, 5, -5, 0])
    if k % 512:
        return np.exp2(np.random.permutation(np.resize(levels, k // 32))).repeat(32)
    a = np.empty((k // 512, 16))
    for p in range(k // 512):
        a[p, :8] = np.random.permutation(np.resize(levels, 8))
        for g in range(8):
            far = levels[np.abs(levels - a[p, g]) >= 10]
            a[p, g + 8] = far[np.random.randint(len(far))]
    return np.exp2(a.ravel()).repeat(32)


def f64(x):
    return np.asarray(x).astype(np.float64)


def striped8(idx):
    return np.concatenate([x.reshape(-1, 16).T for x in idx]).astype(np.uint16)


def runs(offs, k):
    lists = np.stack([offs[16 * r : 16 * r + 16].T.reshape(-1) for r in range(8)]).astype(np.int64)
    return lists[np.arange(k) % 512 // 64]


def pack_weight(w):
    k, n = w.shape
    w = f64(np.asarray(w, np.float32).astype(ml_dtypes.bfloat16)).reshape(k // 32, 32, n)
    amax = np.abs(w).max(1)
    byte = np.clip(np.where(amax > 0, np.frexp(amax)[1] - 1 + 127 - 7, 1), 1, 254)
    scaled = (w * np.exp2(127.0 - byte)[:, None, :]).reshape(k, n).astype(np.float32)
    words = np.ascontiguousarray(scaled.reshape(k // 512, 128, 4, n).transpose(0, 1, 3, 2)).astype(ml_dtypes.float8_e4m3fn).view(np.uint8)
    return words, np.ascontiguousarray(byte.astype(np.uint8).reshape(k // 512, 16, n))


def unpack_weight(words, scales):
    g, p, n, _ = words.shape
    vals = np.ascontiguousarray(words).view(ml_dtypes.float8_e4m3fn).astype(np.float64) * np.repeat(np.exp2(scales.astype(np.float64) - 127.0), 8, axis=1)[..., None]
    return vals.transpose(0, 1, 3, 2).reshape(g * 512, n)


K, T, S, H, W, G, U = 512, 1024, 512, 512, 256, 2048, 1024


def setup_inputs():
    n = np.random.standard_normal
    s = mx_kscale(K)[:, None]
    packed_xT = pack_weight(n((K, T)) * s)
    packed_dT = pack_weight(n((K, G)) / s)
    perm = np.stack([np.random.permutation(S) for _ in range(8)])
    perm2 = np.stack([np.random.permutation(U) for _ in range(8)])
    return {
        "x_words": packed_xT[0],
        "x_scales": packed_xT[1],
        "w1": (n((K, H)) / np.sqrt(K) / s).astype(np.float32),
        "gs": (np.random.uniform(0.5, 1.5, (K, 1)) * s).astype(np.float32),
        "d_words": packed_dT[0],
        "d_scales": packed_dT[1],
        "offs": striped8(np.random.randint(0, T, (8, S))),
        "n1": striped8(perm[:, :W]),
        "n2": striped8(perm[:, W:]),
        "n3": striped8(np.stack([np.random.permutation(S) for _ in range(8)])),
        "k1": striped8(np.random.randint(0, G, (8, H))),
        "k2": striped8(np.random.randint(0, G, (8, H))),
        "hz": striped8(np.random.randint(0, T, (8, S))),
        "n4": striped8(perm2[:, :S]),
        "n5": striped8(perm2[:, S:]),
        "n6": striped8(np.stack([np.random.permutation(S) for _ in range(8)])),
    }


def reference(x_words, x_scales, w1, gs, d_words, d_scales, offs, n1, n2, n3, k1, k2, hz, n4, n5, n6):
    d_k1 = unpack_weight(d_words, d_scales)[np.arange(K)[:, None], runs(k1, K)]
    xq = unpack_weight(x_words, x_scales)[np.arange(K)[:, None], runs(offs, K)]
    y = mxq(f64(w1), 0, "e4m3").T @ xq
    pa = y[np.arange(H)[:, None], runs(n1, H)]
    pb = y[np.arange(H)[:, None], runs(n2, H)]
    rb = pa - pb
    ua = np.zeros((H, S))
    ua[np.arange(H)[:, None], runs(n1, H)] = pb
    ub = ua.copy()
    ub[np.arange(H)[:, None], runs(n2, H)] = rb
    z = f64(gs) * (np.maximum(ub, 0.5 * (ub[np.arange(H)[:, None], runs(n3, H)])))
    d_k2 = unpack_weight(d_words, d_scales)[np.arange(K)[:, None], runs(k2, K)]
    x_hz = unpack_weight(x_words, x_scales)[np.arange(K)[:, None], runs(hz, K)]
    h2 = 0.0625 * ((d_k1.T @ mxq(z, 0, "e4m3") + d_k2.T @ x_hz))
    ds = np.zeros((H, S))
    ds[np.arange(H)[:, None], runs(n6, H)] = h2
    up = np.maximum(h2, ds)
    ph = np.zeros((H, U))
    ph[np.arange(H)[:, None], runs(n4, H)] = ds
    out = ph.copy()
    out[np.arange(H)[:, None], runs(n5, H)] = up
    return out

@@ -1,0 +1,257 @@
+from contextlib import ExitStack
+
+import concourse.mybir as mybir
+
+F32 = mybir.dt.float32
+BF16 = mybir.dt.bfloat16
+I32 = mybir.dt.int32
+U32 = mybir.dt.uint32
+U16 = mybir.dt.uint16
+U8 = mybir.dt.uint8
+FP8X4 = mybir.dt.float8_e4m3fn_x4
+ALU = mybir.AluOpType
+COPY = mybir.ActivationFunctionType.Copy
+
+P = 128
+K, T, S, H, W, G, U = 512, 1024, 512, 512, 256, 2048, 1024
+TILES = 4
+HALF = S // 2
+FLOPS = 3 * 2 * K * H * S
+
+
+def tile_picked_dhzmhswapdpagsn_none_p_kernel(
+    tc, x_words, x_scales, w1, gs, d_words, d_scales, offs, n1, n2, n3, k1, k2, hz, n4, n5, n6, out
+):
+    nc = tc.nc
+    with ExitStack() as ctx:
+        lists = ctx.enter_context(tc.tile_pool(name="lists", bufs=1))
+        keep = ctx.enter_context(tc.tile_pool(name="keep", bufs=1))
+        psum = ctx.enter_context(tc.psum_pool(name="psum", bufs=1))
+
+        def load_list(src, name):
+            tile = lists.tile(list(src.shape), U16, name=name)
+            nc.sync.dma_start(tile[:], src)
+            return tile
+
+        def sb(shape, dtype, name, tag=None):
+            return keep.tile(shape, dtype, name=name, tag=tag or name, align_bytes=64)
+
+        def load_scales(src, width, name):
+            tile = sb([P, width], U8, name)
+            for e in range(2):
+                rows = src[0, e:16:2, :].bitcast(I32).unsqueeze(1).to_broadcast([8, 8, width // 4])
+                nc.sync.dma_start(tile[e:P:2, :].bitcast(I32), rows)
+            return tile
+
+        def load_words(src, width, name):
+            tile = sb([P, width], U32, name)
+            nc.sync.dma_start(tile[:].bitcast(I32), src[0].rearrange("p n t -> p (n t)").bitcast(I32))
+            return tile
+
+        def place_rows(plane, picked):
+            nc.sync.dma_start(plane[:112, :].bitcast(I32), picked[14:126, :].bitcast(I32))
+
+        offs_plane = sb([P, S], U8, "offs_plane")
+        hz_plane = sb([P, S], U8, "hz_plane")
+        d_plane = sb([P, 2 * H], U8, "d_plane")
+        minus_one = sb([P, W], F32, "minus_one")
+        nc.gpsimd.memset(offs_plane[:].bitcast(I32), 0)
+        nc.gpsimd.memset(hz_plane[:].bitcast(I32), 0)
+        nc.gpsimd.memset(d_plane[:].bitcast(I32), 0)
+        nc.gpsimd.memset(minus_one[:], -1.0)
+
+        offs_t = load_list(offs, "offs_t")
+        x_sc = load_scales(x_scales, T, "x_sc")
+        hz_t = load_list(hz, "hz_t")
+        w_raw = []
+        for h in range(2):
+            part = sb([P, 4, H // 2], F32, f"w_raw{h}")
+            nc.sync.dma_start(part[:], w1[:, h * (H // 2) : (h + 1) * (H // 2)].rearrange("(p j) c -> p j c", j=4))
+            w_raw.append(part)
+        x_w = load_words(x_words, T, "x_w")
+        k1_t = load_list(k1, "k1_t")
+        d_sc = load_scales(d_scales, G, "d_sc")
+        k2_t = load_list(k2, "k2_t")
+        n2_t = load_list(n2, "n2_t")
+
+        offs_bytes = sb([P, S], U8, "offs_bytes")
+        nc.vector.tensor_copy(offs_bytes[:], x_sc[:].indirect(offs_t[:]))
+        place_rows(offs_plane, offs_bytes)
+        n1_t = load_list(n1, "n1_t")
+        d_w = load_words(d_words, G, "d_w")
+        hz_bytes = sb([P, S], U8, "hz_bytes")
+        nc.vector.tensor_copy(hz_bytes[:], x_sc[:].indirect(hz_t[:]))
+        place_rows(hz_plane, hz_bytes)
+        x_offs = sb([P, S], U32, "x_offs")
+        nc.vector.tensor_copy(x_offs[:], x_w[:].indirect(offs_t[:]))
+
+        n3_t = load_list(n3, "n3_t")
+        gs_t = sb([P, TILES], F32, "gs_t")
+        nc.sync.dma_start(gs_t[:], gs.rearrange("(p t) o -> p (t o)", t=TILES))
+
+        w_bf = sb([P, 4 * H], BF16, "w_bf")
+        w_view = w_bf[:].rearrange("p (t m j) -> p m t j", t=TILES, j=4)
+        for h in range(2):
+            nc.scalar.copy(w_view[:, 64 * h : 64 * (h + 1)], w_raw[h][:].rearrange("p j (m t) -> p m t j", t=TILES))
+        w_codes = sb([P, H], U32, "w_codes")
+        w_plane = sb([P, H], U8, "w_plane")
+
+        d_bytes = sb([P, 2 * H], U8, "d_bytes")
+        nc.vector.tensor_copy(d_bytes[:, :H], d_sc[:].indirect(k1_t[:]))
+        nc.vector.quantize_mx(out=w_codes[:].bitcast(FP8X4), scales=w_plane[:], in_=w_bf[:])
+        nc.vector.tensor_copy(d_bytes[:, H:], d_sc[:].indirect(k2_t[:]))
+        x_hz = sb([P, S], U32, "x_hz")
+        nc.vector.tensor_copy(x_hz[:], x_w[:].indirect(hz_t[:]))
+        d_k1 = sb([P, H], U32, "d_k1")
+        nc.vector.tensor_copy(d_k1[:], d_w[:].indirect(k1_t[:]))
+        d_bytes_dealt = sb([P, 2 * H], U8, "d_bytes_dealt")
+        nc.vector.tensor_copy(
+            d_bytes_dealt[:].bitcast(I32).rearrange("p (l t g) -> p l t g", l=2, t=TILES),
+            d_bytes[:].bitcast(I32).rearrange("p (l g t) -> p l t g", l=2, t=TILES),
+        )
+        place_rows(d_plane, d_bytes_dealt)
+
+        def deal_words(picked, name):
+            dealt = sb([P, H], U32, name)
+            nc.vector.tensor_copy(
+                dealt[:].bitcast(I32).rearrange("p (t g b) -> p t g b", t=TILES, b=4),
+                picked[:].bitcast(I32).rearrange("p (g t b) -> p t g b", t=TILES, b=4),
+            )
+            return dealt
+
+        n6_t = load_list(n6, "n6_t")
+        n4_t = load_list(n4, "n4_t")
+        n5_t = load_list(n5, "n5_t")
+
+        y = []
+        for t in range(TILES):
+            acc = psum.tile([P, S], F32, name=f"y_acc{t}", tag=f"bank{t}")
+            cols = slice(P * t, P * (t + 1))
+            nc.tensor.matmul_mx(
+                out=acc[:],
+                lhsT=w_codes[:, cols].bitcast(FP8X4),
+                lhsT_scale=w_plane[:, cols],
+                rhs=x_offs[:].bitcast(FP8X4),
+                rhs_scale=offs_plane[:],
+                start=True,
+                stop=True,
+            )
+            y.append(acc)
+
+        y_sb = [sb([P, S], F32, f"y_sb{t}") for t in range(TILES)]
+        neg_pb = [sb([P, W], F32, f"neg_pb{t}") for t in range(TILES)]
+        pa = [sb([P, W], F32, f"pa{t}") for t in range(TILES)]
+        ub = [sb([P, S], F32, f"ub{t}") for t in range(TILES)]
+        far = [sb([P, S], F32, f"far{t}") for t in range(TILES)]
+        top = [sb([P, S], F32, f"top{t}") for t in range(TILES)]
+        z_rows = sb([P, TILES, S], BF16, "z_rows")
+        z_bf = sb([P, S, TILES], BF16, "z_bf")
+        halves = [slice(0, HALF), slice(HALF, S)]
+
+        def evict_y(t):
+            nc.scalar.copy(y_sb[t][:], y[t][:])
+
+        def put_b(t):
+            nc.scalar.activation(neg_pb[t][:], y_sb[t][:].indirect(n2_t[:]), COPY, scale=-1.0)
+            nc.vector.tensor_tensor(ub[t][:].indirect(n1_t[:]), neg_pb[t][:], minus_one[:], ALU.mult)
+
+        def put_a(t):
+            nc.scalar.activation(pa[t][:], y_sb[t][:].indirect(n1_t[:]), COPY)
+            nc.vector.tensor_tensor(ub[t][:].indirect(n2_t[:]), pa[t][:], neg_pb[t][:], ALU.add)
+
+        def take_max(t):
+            for h in range(2):
+                nc.scalar.activation(far[t][:, halves[h]], ub[t][:].indirect(n3_t[:, 16 * h : 16 * (h + 1)]), COPY)
+            for cols in halves if t == TILES - 1 else [slice(0, S)]:
+                nc.vector.scalar_tensor_tensor(top[t][:, cols], far[t][:, cols], 0.5, ub[t][:, cols], ALU.mult, ALU.max)
+
+        def weigh(t):
+            for cols in halves if t == TILES - 1 else [slice(0, S)]:
+                nc.scalar.activation(z_rows[:, t, cols], top[t][:, cols], COPY, scale=gs_t[:, t : t + 1])
+
+        evict_y(0)
+        put_b(0)
+        d_k1_dealt = deal_words(d_k1, "d_k1_dealt")
+        evict_y(1)
+        put_b(1)
+        put_a(0)
+        evict_y(2)
+        put_b(2)
+        put_a(1)
+        evict_y(3)
+        take_max(0)
+        put_b(3)
+        put_a(2)
+        take_max(1)
+        weigh(0)
+        put_a(3)
+        take_max(2)
+        weigh(1)
+        d_k2 = sb([P, H], U32, "d_k2", tag=f"pa{TILES - 1}")
+        nc.vector.tensor_copy(d_k2[:], d_w[:].indirect(k2_t[:]))
+        take_max(3)
+        weigh(2)
+        weigh(3)
+        d_k2_dealt = deal_words(d_k2, "d_k2_dealt")
+
+        z_codes = sb([P, S], U32, "z_codes")
+        z_plane = sb([P, S], U8, "z_plane")
+        for cols in halves:
+            nc.vector.tensor_copy(
+                z_bf[:, cols, :].rearrange("p (c i) t -> p c t i", i=4),
+                z_rows[:, :, cols].rearrange("p t (c i) -> p c t i", i=4),
+            )
+        for cols in halves:
+            nc.vector.quantize_mx(
+                out=z_codes[:, cols].bitcast(FP8X4),
+                scales=z_plane[:, cols],
+                in_=z_bf[:, cols, :].rearrange("p c t -> p (c t)"),
+            )
+
+        h2 = [sb([P, S], F32, f"h2_{t}") for t in range(TILES)]
+        ds_up = [sb([P, 2 * S], F32, f"ds_up{t}") for t in range(TILES)]
+        page = [sb([P, U], F32, f"page{t}") for t in range(TILES)]
+        out_rows = out.rearrange("(g t b) w -> t g b w", t=TILES, b=4)
+
+        def second_product(t, lo, hi, bank):
+            acc = psum.tile([P, hi - lo], F32, name=f"h_acc{t}_{lo}", tag=f"bank{bank}")
+            m = slice(P * t, P * (t + 1))
+            nc.tensor.matmul_mx(
+                out=acc[:],
+                lhsT=d_k2_dealt[:, m].bitcast(FP8X4),
+                lhsT_scale=d_plane[:, H + P * t : H + P * (t + 1)],
+                rhs=x_hz[:, lo:hi].bitcast(FP8X4),
+                rhs_scale=hz_plane[:, lo:hi],
+                start=True,
+                stop=False,
+            )
+            nc.tensor.matmul_mx(
+                out=acc[:],
+                lhsT=d_k1_dealt[:, m].bitcast(FP8X4),
+                lhsT_scale=d_plane[:, m],
+                rhs=z_codes[:, lo:hi].bitcast(FP8X4),
+                rhs_scale=z_plane[:, lo:hi],
+                start=False,
+                stop=True,
+            )
+            nc.scalar.activation(h2[t][:, lo:hi], acc[:], COPY, scale=0.0625)
+            nc.vector.tensor_copy(ds_up[t][:].indirect(n6_t[:, lo // 16 : hi // 16]), h2[t][:, lo:hi])
+
+        def put_ds(t):
+            nc.vector.tensor_copy(page[t][:].indirect(n4_t[:]), ds_up[t][:, :S])
+            nc.vector.tensor_tensor(ds_up[t][:, S:], ds_up[t][:, :S], h2[t][:], ALU.max)
+
+        def put_up(t):
+            nc.vector.tensor_copy(page[t][:].indirect(n5_t[:]), ds_up[t][:, S:])
+            nc.sync.dma_start(out_rows[t], page[t][:])
+
+        second_product(0, 0, HALF, 4)
+        second_product(0, HALF, S, 5)
+        second_product(1, 0, S, 6)
+        for t in range(TILES):
+            put_ds(t)
+            if t + 2 < TILES:
+                second_product(t + 2, 0, S, (7, 0)[t])
+            if t > 0:
+                put_up(t - 1)
+        put_up(TILES - 1)

@@ -1,6 +1,7 @@
 from contextlib import ExitStack
 
 import concourse.mybir as mybir
+from concourse.masks import make_identity
 
 F32 = mybir.dt.float32
 BF16 = mybir.dt.bfloat16
@@ -11,6 +12,7 @@ U8 = mybir.dt.uint8
 FP8X4 = mybir.dt.float8_e4m3fn_x4
 ALU = mybir.AluOpType
 COPY = mybir.ActivationFunctionType.Copy
+RELU = mybir.ActivationFunctionType.Relu
 
 P = 128
 K, T, S, H, W, G, U = 512, 1024, 512, 512, 256, 2048, 1024
@@ -43,13 +45,16 @@ def tile_picked_dhzmhswapdpagsn_none_p_kernel(
                 nc.sync.dma_start(tile[e:P:2, :].bitcast(I32), rows)
             return tile
 
-        def load_words(src, width, name):
+        def load_words(src, width, name, parts):
             tile = sb([P, width], U32, name)
-            nc.sync.dma_start(tile[:].bitcast(I32), src[0].rearrange("p n t -> p (n t)").bitcast(I32))
+            words = src[0].rearrange("p n t -> p (n t)").bitcast(I32)
+            for lo in range(0, width, width // parts):
+                cols = slice(lo, lo + width // parts)
+                nc.sync.dma_start(tile[:, cols].bitcast(I32), words[:, cols])
             return tile
 
         def place_rows(plane, picked):
-            nc.sync.dma_start(plane[:112, :].bitcast(I32), picked[14:126, :].bitcast(I32))
+            nc.gpsimd.dma_start(plane[:112, :].bitcast(I32), picked[14:126, :].bitcast(I32))
 
         offs_plane = sb([P, S], U8, "offs_plane")
         hz_plane = sb([P, S], U8, "hz_plane")
@@ -59,35 +64,46 @@ def tile_picked_dhzmhswapdpagsn_none_p_kernel(
         nc.gpsimd.memset(hz_plane[:].bitcast(I32), 0)
         nc.gpsimd.memset(d_plane[:].bitcast(I32), 0)
         nc.gpsimd.memset(minus_one[:], -1.0)
+        identity = sb([P, P], F32, "identity")
+        make_identity(nc, identity[:])
+
+        def load_w(h):
+            part = sb([P, 4, H // 2], F32, f"w_raw{h}")
+            nc.sync.dma_start(part[:], w1[:, h * (H // 2) : (h + 1) * (H // 2)].rearrange("(p j) c -> p j c", j=4))
+            return part
 
         offs_t = load_list(offs, "offs_t")
         x_sc = load_scales(x_scales, T, "x_sc")
         hz_t = load_list(hz, "hz_t")
-        w_raw = []
-        for h in range(2):
-            part = sb([P, 4, H // 2], F32, f"w_raw{h}")
-            nc.sync.dma_start(part[:], w1[:, h * (H // 2) : (h + 1) * (H // 2)].rearrange("(p j) c -> p j c", j=4))
-            w_raw.append(part)
-        x_w = load_words(x_words, T, "x_w")
+        x_w = load_words(x_words, T, "x_w", 1)
         k1_t = load_list(k1, "k1_t")
         d_sc = load_scales(d_scales, G, "d_sc")
+        w_raw = [load_w(0)]
         k2_t = load_list(k2, "k2_t")
+        w_raw.append(load_w(1))
         n2_t = load_list(n2, "n2_t")
+        d_w = load_words(d_words, G, "d_w", 4)
+        n1_t = load_list(n1, "n1_t")
+        n3_t = load_list(n3, "n3_t")
+        gs_t = sb([P, TILES], F32, "gs_t")
+        nc.sync.dma_start(gs_t[:], gs.rearrange("(p t) o -> p (t o)", t=TILES))
+        n6_t = load_list(n6, "n6_t")
+        n4_t = load_list(n4, "n4_t")
+        n5_t = load_list(n5, "n5_t")
 
         offs_bytes = sb([P, S], U8, "offs_bytes")
         nc.vector.tensor_copy(offs_bytes[:], x_sc[:].indirect(offs_t[:]))
         place_rows(offs_plane, offs_bytes)
-        n1_t = load_list(n1, "n1_t")
-        d_w = load_words(d_words, G, "d_w")
         hz_bytes = sb([P, S], U8, "hz_bytes")
         nc.vector.tensor_copy(hz_bytes[:], x_sc[:].indirect(hz_t[:]))
         place_rows(hz_plane, hz_bytes)
         x_offs = sb([P, S], U32, "x_offs")
         nc.vector.tensor_copy(x_offs[:], x_w[:].indirect(offs_t[:]))
-
-        n3_t = load_list(n3, "n3_t")
-        gs_t = sb([P, TILES], F32, "gs_t")
-        nc.sync.dma_start(gs_t[:], gs.rearrange("(p t) o -> p (t o)", t=TILES))
+        x_hz = [sb([P, HALF], U32, "x_hz0")]
+        nc.vector.tensor_copy(x_hz[0][:], x_w[:].indirect(hz_t[:, :16]))
+        d_bytes = sb([P, 2 * H], U8, "d_bytes")
+        nc.vector.tensor_copy(d_bytes[:, :H], d_sc[:].indirect(k1_t[:]))
+        nc.vector.tensor_copy(d_bytes[:, H:], d_sc[:].indirect(k2_t[:]))
 
         w_bf = sb([P, 4 * H], BF16, "w_bf")
         w_view = w_bf[:].rearrange("p (t m j) -> p m t j", t=TILES, j=4)
@@ -95,33 +111,27 @@ def tile_picked_dhzmhswapdpagsn_none_p_kernel(
             nc.scalar.copy(w_view[:, 64 * h : 64 * (h + 1)], w_raw[h][:].rearrange("p j (m t) -> p m t j", t=TILES))
         w_codes = sb([P, H], U32, "w_codes")
         w_plane = sb([P, H], U8, "w_plane")
+        for lo, hi in ((0, P), (P, H)):
+            nc.vector.quantize_mx(
+                out=w_codes[:, lo:hi].bitcast(FP8X4), scales=w_plane[:, lo:hi], in_=w_bf[:, 4 * lo : 4 * hi]
+            )
 
-        d_bytes = sb([P, 2 * H], U8, "d_bytes")
-        nc.vector.tensor_copy(d_bytes[:, :H], d_sc[:].indirect(k1_t[:]))
-        nc.vector.quantize_mx(out=w_codes[:].bitcast(FP8X4), scales=w_plane[:], in_=w_bf[:])
-        nc.vector.tensor_copy(d_bytes[:, H:], d_sc[:].indirect(k2_t[:]))
-        x_hz = sb([P, S], U32, "x_hz")
-        nc.vector.tensor_copy(x_hz[:], x_w[:].indirect(hz_t[:]))
-        d_k1 = sb([P, H], U32, "d_k1")
-        nc.vector.tensor_copy(d_k1[:], d_w[:].indirect(k1_t[:]))
-        d_bytes_dealt = sb([P, 2 * H], U8, "d_bytes_dealt")
+        d_bytes_dealt = sb([P, 2 * H], U8, "d_bytes_dealt", tag="w_raw1")
         nc.vector.tensor_copy(
             d_bytes_dealt[:].bitcast(I32).rearrange("p (l t g) -> p l t g", l=2, t=TILES),
             d_bytes[:].bitcast(I32).rearrange("p (l g t) -> p l t g", l=2, t=TILES),
         )
         place_rows(d_plane, d_bytes_dealt)
+        d_k1 = sb([P, H], U32, "d_k1")
+        nc.vector.tensor_copy(d_k1[:], d_w[:].indirect(k1_t[:]))
 
-        def deal_words(picked, name):
-            dealt = sb([P, H], U32, name)
+        def deal_words(picked, name, tag=None):
+            dealt = sb([P, H], U32, name, tag)
             nc.vector.tensor_copy(
                 dealt[:].bitcast(I32).rearrange("p (t g b) -> p t g b", t=TILES, b=4),
                 picked[:].bitcast(I32).rearrange("p (g t b) -> p t g b", t=TILES, b=4),
             )
             return dealt
-
-        n6_t = load_list(n6, "n6_t")
-        n4_t = load_list(n4, "n4_t")
-        n5_t = load_list(n5, "n5_t")
 
         y = []
         for t in range(TILES):
@@ -141,11 +151,12 @@ def tile_picked_dhzmhswapdpagsn_none_p_kernel(
         y_sb = [sb([P, S], F32, f"y_sb{t}") for t in range(TILES)]
         neg_pb = [sb([P, W], F32, f"neg_pb{t}") for t in range(TILES)]
         pa = [sb([P, W], F32, f"pa{t}") for t in range(TILES)]
+        d_k1_dealt = deal_words(d_k1, "d_k1_dealt")
         ub = [sb([P, S], F32, f"ub{t}") for t in range(TILES)]
         far = [sb([P, S], F32, f"far{t}") for t in range(TILES)]
         top = [sb([P, S], F32, f"top{t}") for t in range(TILES)]
         z_rows = sb([P, TILES, S], BF16, "z_rows")
-        z_bf = sb([P, S, TILES], BF16, "z_bf")
+        z_bf = [sb([P, HALF, TILES], BF16, f"z_bf{h}") for h in range(2)]
         halves = [slice(0, HALF), slice(HALF, S)]
 
         def evict_y(t):
@@ -171,7 +182,6 @@ def tile_picked_dhzmhswapdpagsn_none_p_kernel(
 
         evict_y(0)
         put_b(0)
-        d_k1_dealt = deal_words(d_k1, "d_k1_dealt")
         evict_y(1)
         put_b(1)
         put_a(0)
@@ -180,48 +190,58 @@ def tile_picked_dhzmhswapdpagsn_none_p_kernel(
         put_a(1)
         evict_y(3)
         take_max(0)
-        put_b(3)
         put_a(2)
         take_max(1)
+        put_b(3)
+        take_max(2)
         weigh(0)
         put_a(3)
-        take_max(2)
         weigh(1)
+        weigh(2)
         d_k2 = sb([P, H], U32, "d_k2", tag=f"pa{TILES - 1}")
         nc.vector.tensor_copy(d_k2[:], d_w[:].indirect(k2_t[:]))
         take_max(3)
-        weigh(2)
         weigh(3)
-        d_k2_dealt = deal_words(d_k2, "d_k2_dealt")
+        d_k2_dealt = deal_words(d_k2, "d_k2_dealt", f"far{TILES - 1}")
 
         z_codes = sb([P, S], U32, "z_codes")
         z_plane = sb([P, S], U8, "z_plane")
-        for cols in halves:
-            nc.vector.tensor_copy(
-                z_bf[:, cols, :].rearrange("p (c i) t -> p c t i", i=4),
-                z_rows[:, :, cols].rearrange("p t (c i) -> p c t i", i=4),
+        for h, move in enumerate((nc.vector.tensor_copy, nc.scalar.copy)):
+            move(
+                z_bf[h][:].rearrange("p (c i) t -> p c t i", i=4),
+                z_rows[:, :, halves[h]].rearrange("p t (c i) -> p c t i", i=4),
             )
-        for cols in halves:
+
+        def quantise_z(h):
             nc.vector.quantize_mx(
-                out=z_codes[:, cols].bitcast(FP8X4),
-                scales=z_plane[:, cols],
-                in_=z_bf[:, cols, :].rearrange("p c t -> p (c t)"),
+                out=z_codes[:, halves[h]].bitcast(FP8X4),
+                scales=z_plane[:, halves[h]],
+                in_=z_bf[h][:].rearrange("p c t -> p (c t)"),
             )
+
+        quantise_z(0)
+        x_hz.append(sb([P, HALF], U32, "x_hz1", tag="z_bf0"))
+        nc.vector.tensor_copy(x_hz[1][:], x_w[:].indirect(hz_t[:, 16:]))
+        quantise_z(1)
 
         h2 = [sb([P, S], F32, f"h2_{t}") for t in range(TILES)]
-        ds_up = [sb([P, 2 * S], F32, f"ds_up{t}") for t in range(TILES)]
-        page = [sb([P, U], F32, f"page{t}") for t in range(TILES)]
+        neg_h2 = [sb([P, S], F32, f"neg_h2_{t}", tag=f"page{t}") for t in range(TILES)]
+        ds_gain = [sb([P, 2 * S], F32, f"ds_gain{t}") for t in range(TILES)]
+        gain_turned = [sb([P, S], F32, f"gain_turned{t}") for t in range(TILES)]
         out_rows = out.rearrange("(g t b) w -> t g b w", t=TILES, b=4)
+        h_acc = {}
+        page = {}
 
-        def second_product(t, lo, hi, bank):
-            acc = psum.tile([P, hi - lo], F32, name=f"h_acc{t}_{lo}", tag=f"bank{bank}")
+        def second_product(t, h):
+            acc = psum.tile([P, HALF], F32, name=f"h_acc{t}_{h}", tag=f"bank{(4 + 2 * (t % 2) + h)}")
             m = slice(P * t, P * (t + 1))
+            cols = halves[h]
             nc.tensor.matmul_mx(
                 out=acc[:],
                 lhsT=d_k2_dealt[:, m].bitcast(FP8X4),
                 lhsT_scale=d_plane[:, H + P * t : H + P * (t + 1)],
-                rhs=x_hz[:, lo:hi].bitcast(FP8X4),
-                rhs_scale=hz_plane[:, lo:hi],
+                rhs=x_hz[h][:].bitcast(FP8X4),
+                rhs_scale=hz_plane[:, cols],
                 start=True,
                 stop=False,
             )
@@ -229,29 +249,59 @@ def tile_picked_dhzmhswapdpagsn_none_p_kernel(
                 out=acc[:],
                 lhsT=d_k1_dealt[:, m].bitcast(FP8X4),
                 lhsT_scale=d_plane[:, m],
-                rhs=z_codes[:, lo:hi].bitcast(FP8X4),
-                rhs_scale=z_plane[:, lo:hi],
+                rhs=z_codes[:, cols].bitcast(FP8X4),
+                rhs_scale=z_plane[:, cols],
                 start=False,
                 stop=True,
             )
-            nc.scalar.activation(h2[t][:, lo:hi], acc[:], COPY, scale=0.0625)
-            nc.vector.tensor_copy(ds_up[t][:].indirect(n6_t[:, lo // 16 : hi // 16]), h2[t][:, lo:hi])
+            nc.scalar.activation(h2[t][:, cols], acc[:], COPY, scale=0.0625)
+            h_acc[t, h] = acc
+
+        def negate(t):
+            for h in range(2):
+                nc.scalar.activation(neg_h2[t][:, halves[h]], h_acc[t, h][:], COPY, scale=-0.0625)
+
+        def put_h2(t, lo, hi):
+            nc.vector.tensor_copy(ds_gain[t][:].indirect(n6_t[:, lo // 16 : hi // 16]), h2[t][:, lo:hi])
+
+        def make_gain(t):
+            diff = psum.tile([P, S], F32, name=f"diff{t}", tag=f"bank{t % 2}")
+            for c in range(S // P):
+                cols = slice(P * c, P * (c + 1))
+                nc.tensor.matmul(diff[:, cols], ds_gain[t][:, cols], identity[:], start=True, stop=False, is_transpose=True)
+                nc.tensor.matmul(diff[:, cols], neg_h2[t][:, cols], identity[:], start=False, stop=True, is_transpose=True)
+            nc.scalar.activation(gain_turned[t][:], diff[:], RELU)
+            back = psum.tile([P, S], F32, name=f"back{t}", tag=f"bank{2 + t % 2}")
+            for c in range(S // P):
+                cols = slice(P * c, P * (c + 1))
+                nc.tensor.transpose(back[:, cols], gain_turned[t][:, cols], identity[:])
+            nc.scalar.copy(ds_gain[t][:, S:], back[:])
 
         def put_ds(t):
-            nc.vector.tensor_copy(page[t][:].indirect(n4_t[:]), ds_up[t][:, :S])
-            nc.vector.tensor_tensor(ds_up[t][:, S:], ds_up[t][:, :S], h2[t][:], ALU.max)
+            page[t] = sb([P, U], F32, f"page{t}")
+            nc.vector.tensor_copy(page[t][:].indirect(n4_t[:]), ds_gain[t][:, :S])
 
         def put_up(t):
-            nc.vector.tensor_copy(page[t][:].indirect(n5_t[:]), ds_up[t][:, S:])
+            nc.vector.tensor_tensor(page[t][:].indirect(n5_t[:]), h2[t][:], ds_gain[t][:, S:], ALU.add)
             nc.sync.dma_start(out_rows[t], page[t][:])
 
-        second_product(0, 0, HALF, 4)
-        second_product(0, HALF, S, 5)
-        second_product(1, 0, S, 6)
-        for t in range(TILES):
+        for h in range(2):
+            for t in range(2):
+                second_product(t, h)
+                put_h2(t, HALF * h, HALF * (h + 1))
+        for t in range(2):
+            negate(t)
+        for t in range(2):
+            make_gain(t)
             put_ds(t)
-            if t + 2 < TILES:
-                second_product(t + 2, 0, S, (7, 0)[t])
-            if t > 0:
-                put_up(t - 1)
-        put_up(TILES - 1)
+        for t in range(2, TILES):
+            for h in range(2):
+                second_product(t, h)
+            negate(t)
+            put_h2(t, 0, S)
+            put_up(t - 2)
+            make_gain(t)
+        for t in range(2, TILES):
+            put_ds(t)
+        for t in range(2, TILES):
+            put_up(t)

@@ -72,8 +72,8 @@ def tile_picked_dhzmhswapdpagsn_none_p_kernel(
             nc.sync.dma_start(part[:], w1[:, h * (H // 2) : (h + 1) * (H // 2)].rearrange("(p j) c -> p j c", j=4))
             return part
 
-        offs_t = load_list(offs, "offs_t")
         x_sc = load_scales(x_scales, T, "x_sc")
+        offs_t = load_list(offs, "offs_t")
         hz_t = load_list(hz, "hz_t")
         x_w = load_words(x_words, T, "x_w", 1)
         k1_t = load_list(k1, "k1_t")
@@ -191,8 +191,8 @@ def tile_picked_dhzmhswapdpagsn_none_p_kernel(
         evict_y(3)
         take_max(0)
         put_a(2)
-        take_max(1)
         put_b(3)
+        take_max(1)
         take_max(2)
         weigh(0)
         put_a(3)
@@ -225,7 +225,7 @@ def tile_picked_dhzmhswapdpagsn_none_p_kernel(
         quantise_z(1)
 
         h2 = [sb([P, S], F32, f"h2_{t}") for t in range(TILES)]
-        neg_h2 = [sb([P, S], F32, f"neg_h2_{t}", tag=f"page{t}") for t in range(TILES)]
+        neg_h2 = [sb([P, S], F32, f"neg_h2_{t}", tag=f"page{t}" if t > 0 else None) for t in range(TILES)]
         ds_gain = [sb([P, 2 * S], F32, f"ds_gain{t}") for t in range(TILES)]
         gain_turned = [sb([P, S], F32, f"gain_turned{t}") for t in range(TILES)]
         out_rows = out.rearrange("(g t b) w -> t g b w", t=TILES, b=4)

from contextlib import ExitStack

import concourse.mybir as mybir
from concourse.masks import make_identity

F32 = mybir.dt.float32
BF16 = mybir.dt.bfloat16
I32 = mybir.dt.int32
U32 = mybir.dt.uint32
U16 = mybir.dt.uint16
U8 = mybir.dt.uint8
FP8X4 = mybir.dt.float8_e4m3fn_x4
ALU = mybir.AluOpType
COPY = mybir.ActivationFunctionType.Copy
RELU = mybir.ActivationFunctionType.Relu

P = 128
K, T, S, H, W, G, U = 512, 1024, 512, 512, 256, 2048, 1024
TILES = 4
HALF = S // 2
FLOPS = 3 * 2 * K * H * S


def tile_picked_dhzmhswapdpagsn_none_p_kernel(
    tc, x_words, x_scales, w1, gs, d_words, d_scales, offs, n1, n2, n3, k1, k2, hz, n4, n5, n6, out
):
    nc = tc.nc
    with ExitStack() as ctx:
        lists = ctx.enter_context(tc.tile_pool(name="lists", bufs=1))
        keep = ctx.enter_context(tc.tile_pool(name="keep", bufs=1))
        psum = ctx.enter_context(tc.psum_pool(name="psum", bufs=1))

        def load_list(src, name):
            tile = lists.tile(list(src.shape), U16, name=name)
            nc.sync.dma_start(tile[:], src)
            return tile

        def sb(shape, dtype, name, tag=None):
            return keep.tile(shape, dtype, name=name, tag=tag or name, align_bytes=64)

        def load_scales(src, width, name):
            tile = sb([P, width], U8, name)
            for e in range(2):
                rows = src[0, e:16:2, :].bitcast(I32).unsqueeze(1).to_broadcast([8, 8, width // 4])
                nc.sync.dma_start(tile[e:P:2, :].bitcast(I32), rows)
            return tile

        def load_words(src, width, name, parts):
            tile = sb([P, width], U32, name)
            words = src[0].rearrange("p n t -> p (n t)").bitcast(I32)
            for lo in range(0, width, width // parts):
                cols = slice(lo, lo + width // parts)
                nc.sync.dma_start(tile[:, cols].bitcast(I32), words[:, cols])
            return tile

        def place_rows(plane, picked):
            nc.gpsimd.dma_start(plane[:112, :].bitcast(I32), picked[14:126, :].bitcast(I32))

        offs_plane = sb([P, S], U8, "offs_plane")
        hz_plane = sb([P, S], U8, "hz_plane")
        d_plane = sb([P, 2 * H], U8, "d_plane")
        minus_one = sb([P, W], F32, "minus_one")
        nc.gpsimd.memset(offs_plane[:].bitcast(I32), 0)
        nc.gpsimd.memset(hz_plane[:].bitcast(I32), 0)
        nc.gpsimd.memset(d_plane[:].bitcast(I32), 0)
        nc.gpsimd.memset(minus_one[:], -1.0)
        identity = sb([P, P], F32, "identity")
        make_identity(nc, identity[:])

        def load_w(h):
            part = sb([P, 4, H // 2], F32, f"w_raw{h}")
            nc.sync.dma_start(part[:], w1[:, h * (H // 2) : (h + 1) * (H // 2)].rearrange("(p j) c -> p j c", j=4))
            return part

        x_sc = load_scales(x_scales, T, "x_sc")
        offs_t = load_list(offs, "offs_t")
        hz_t = load_list(hz, "hz_t")
        x_w = load_words(x_words, T, "x_w", 1)
        k1_t = load_list(k1, "k1_t")
        d_sc = load_scales(d_scales, G, "d_sc")
        w_raw = [load_w(0)]
        k2_t = load_list(k2, "k2_t")
        w_raw.append(load_w(1))
        n2_t = load_list(n2, "n2_t")
        d_w = load_words(d_words, G, "d_w", 4)
        n1_t = load_list(n1, "n1_t")
        n3_t = load_list(n3, "n3_t")
        gs_t = sb([P, TILES], F32, "gs_t")
        nc.sync.dma_start(gs_t[:], gs.rearrange("(p t) o -> p (t o)", t=TILES))
        n6_t = load_list(n6, "n6_t")
        n4_t = load_list(n4, "n4_t")
        n5_t = load_list(n5, "n5_t")

        offs_bytes = sb([P, S], U8, "offs_bytes")
        nc.vector.tensor_copy(offs_bytes[:], x_sc[:].indirect(offs_t[:]))
        place_rows(offs_plane, offs_bytes)
        hz_bytes = sb([P, S], U8, "hz_bytes")
        nc.vector.tensor_copy(hz_bytes[:], x_sc[:].indirect(hz_t[:]))
        place_rows(hz_plane, hz_bytes)
        x_offs = sb([P, S], U32, "x_offs")
        nc.vector.tensor_copy(x_offs[:], x_w[:].indirect(offs_t[:]))
        x_hz = [sb([P, HALF], U32, "x_hz0")]
        nc.vector.tensor_copy(x_hz[0][:], x_w[:].indirect(hz_t[:, :16]))
        d_bytes = sb([P, 2 * H], U8, "d_bytes")
        nc.vector.tensor_copy(d_bytes[:, :H], d_sc[:].indirect(k1_t[:]))
        nc.vector.tensor_copy(d_bytes[:, H:], d_sc[:].indirect(k2_t[:]))

        w_bf = sb([P, 4 * H], BF16, "w_bf")
        w_view = w_bf[:].rearrange("p (t m j) -> p m t j", t=TILES, j=4)
        for h in range(2):
            nc.scalar.copy(w_view[:, 64 * h : 64 * (h + 1)], w_raw[h][:].rearrange("p j (m t) -> p m t j", t=TILES))
        w_codes = sb([P, H], U32, "w_codes")
        w_plane = sb([P, H], U8, "w_plane")
        for lo, hi in ((0, P), (P, H)):
            nc.vector.quantize_mx(
                out=w_codes[:, lo:hi].bitcast(FP8X4), scales=w_plane[:, lo:hi], in_=w_bf[:, 4 * lo : 4 * hi]
            )

        d_bytes_dealt = sb([P, 2 * H], U8, "d_bytes_dealt", tag="w_raw1")
        nc.vector.tensor_copy(
            d_bytes_dealt[:].bitcast(I32).rearrange("p (l t g) -> p l t g", l=2, t=TILES),
            d_bytes[:].bitcast(I32).rearrange("p (l g t) -> p l t g", l=2, t=TILES),
        )
        place_rows(d_plane, d_bytes_dealt)
        d_k1 = sb([P, H], U32, "d_k1")
        nc.vector.tensor_copy(d_k1[:], d_w[:].indirect(k1_t[:]))

        def deal_words(picked, name, tag=None):
            dealt = sb([P, H], U32, name, tag)
            nc.vector.tensor_copy(
                dealt[:].bitcast(I32).rearrange("p (t g b) -> p t g b", t=TILES, b=4),
                picked[:].bitcast(I32).rearrange("p (g t b) -> p t g b", t=TILES, b=4),
            )
            return dealt

        y = []
        for t in range(TILES):
            acc = psum.tile([P, S], F32, name=f"y_acc{t}", tag=f"bank{t}")
            cols = slice(P * t, P * (t + 1))
            nc.tensor.matmul_mx(
                out=acc[:],
                lhsT=w_codes[:, cols].bitcast(FP8X4),
                lhsT_scale=w_plane[:, cols],
                rhs=x_offs[:].bitcast(FP8X4),
                rhs_scale=offs_plane[:],
                start=True,
                stop=True,
            )
            y.append(acc)

        y_sb = [sb([P, S], F32, f"y_sb{t}") for t in range(TILES)]
        neg_pb = [sb([P, W], F32, f"neg_pb{t}") for t in range(TILES)]
        pa = [sb([P, W], F32, f"pa{t}") for t in range(TILES)]
        d_k1_dealt = deal_words(d_k1, "d_k1_dealt")
        ub = [sb([P, S], F32, f"ub{t}") for t in range(TILES)]
        far = [sb([P, S], F32, f"far{t}") for t in range(TILES)]
        top = [sb([P, S], F32, f"top{t}") for t in range(TILES)]
        z_rows = sb([P, TILES, S], BF16, "z_rows")
        z_bf = [sb([P, HALF, TILES], BF16, f"z_bf{h}") for h in range(2)]
        halves = [slice(0, HALF), slice(HALF, S)]

        def evict_y(t):
            nc.scalar.copy(y_sb[t][:], y[t][:])

        def put_b(t):
            nc.scalar.activation(neg_pb[t][:], y_sb[t][:].indirect(n2_t[:]), COPY, scale=-1.0)
            nc.vector.tensor_tensor(ub[t][:].indirect(n1_t[:]), neg_pb[t][:], minus_one[:], ALU.mult)

        def put_a(t):
            nc.scalar.activation(pa[t][:], y_sb[t][:].indirect(n1_t[:]), COPY)
            nc.vector.tensor_tensor(ub[t][:].indirect(n2_t[:]), pa[t][:], neg_pb[t][:], ALU.add)

        def take_max(t):
            for h in range(2):
                nc.scalar.activation(far[t][:, halves[h]], ub[t][:].indirect(n3_t[:, 16 * h : 16 * (h + 1)]), COPY)
            for cols in halves if t == TILES - 1 else [slice(0, S)]:
                nc.vector.scalar_tensor_tensor(top[t][:, cols], far[t][:, cols], 0.5, ub[t][:, cols], ALU.mult, ALU.max)

        def weigh(t):
            for cols in halves if t == TILES - 1 else [slice(0, S)]:
                nc.scalar.activation(z_rows[:, t, cols], top[t][:, cols], COPY, scale=gs_t[:, t : t + 1])

        evict_y(0)
        put_b(0)
        evict_y(1)
        put_b(1)
        put_a(0)
        evict_y(2)
        put_b(2)
        put_a(1)
        evict_y(3)
        take_max(0)
        put_a(2)
        put_b(3)
        take_max(1)
        take_max(2)
        weigh(0)
        put_a(3)
        weigh(1)
        weigh(2)
        d_k2 = sb([P, H], U32, "d_k2", tag=f"pa{TILES - 1}")
        nc.vector.tensor_copy(d_k2[:], d_w[:].indirect(k2_t[:]))
        take_max(3)
        weigh(3)
        d_k2_dealt = deal_words(d_k2, "d_k2_dealt", f"far{TILES - 1}")

        z_codes = sb([P, S], U32, "z_codes")
        z_plane = sb([P, S], U8, "z_plane")
        for h, move in enumerate((nc.vector.tensor_copy, nc.scalar.copy)):
            move(
                z_bf[h][:].rearrange("p (c i) t -> p c t i", i=4),
                z_rows[:, :, halves[h]].rearrange("p t (c i) -> p c t i", i=4),
            )

        def quantise_z(h):
            nc.vector.quantize_mx(
                out=z_codes[:, halves[h]].bitcast(FP8X4),
                scales=z_plane[:, halves[h]],
                in_=z_bf[h][:].rearrange("p c t -> p (c t)"),
            )

        quantise_z(0)
        x_hz.append(sb([P, HALF], U32, "x_hz1", tag="z_bf0"))
        nc.vector.tensor_copy(x_hz[1][:], x_w[:].indirect(hz_t[:, 16:]))
        quantise_z(1)

        h2 = [sb([P, S], F32, f"h2_{t}") for t in range(TILES)]
        neg_h2 = [sb([P, S], F32, f"neg_h2_{t}", tag=f"page{t}" if t > 0 else None) for t in range(TILES)]
        ds_gain = [sb([P, 2 * S], F32, f"ds_gain{t}") for t in range(TILES)]
        gain_turned = [sb([P, S], F32, f"gain_turned{t}") for t in range(TILES)]
        out_rows = out.rearrange("(g t b) w -> t g b w", t=TILES, b=4)
        h_acc = {}
        page = {}

        def second_product(t, h):
            acc = psum.tile([P, HALF], F32, name=f"h_acc{t}_{h}", tag=f"bank{(4 + 2 * (t % 2) + h)}")
            m = slice(P * t, P * (t + 1))
            cols = halves[h]
            nc.tensor.matmul_mx(
                out=acc[:],
                lhsT=d_k2_dealt[:, m].bitcast(FP8X4),
                lhsT_scale=d_plane[:, H + P * t : H + P * (t + 1)],
                rhs=x_hz[h][:].bitcast(FP8X4),
                rhs_scale=hz_plane[:, cols],
                start=True,
                stop=False,
            )
            nc.tensor.matmul_mx(
                out=acc[:],
                lhsT=d_k1_dealt[:, m].bitcast(FP8X4),
                lhsT_scale=d_plane[:, m],
                rhs=z_codes[:, cols].bitcast(FP8X4),
                rhs_scale=z_plane[:, cols],
                start=False,
                stop=True,
            )
            nc.scalar.activation(h2[t][:, cols], acc[:], COPY, scale=0.0625)
            h_acc[t, h] = acc

        def negate(t):
            for h in range(2):
                nc.scalar.activation(neg_h2[t][:, halves[h]], h_acc[t, h][:], COPY, scale=-0.0625)

        def put_h2(t, lo, hi):
            nc.vector.tensor_copy(ds_gain[t][:].indirect(n6_t[:, lo // 16 : hi // 16]), h2[t][:, lo:hi])

        def make_gain(t):
            diff = psum.tile([P, S], F32, name=f"diff{t}", tag=f"bank{t % 2}")
            for c in range(S // P):
                cols = slice(P * c, P * (c + 1))
                nc.tensor.matmul(diff[:, cols], ds_gain[t][:, cols], identity[:], start=True, stop=False, is_transpose=True)
                nc.tensor.matmul(diff[:, cols], neg_h2[t][:, cols], identity[:], start=False, stop=True, is_transpose=True)
            nc.scalar.activation(gain_turned[t][:], diff[:], RELU)
            back = psum.tile([P, S], F32, name=f"back{t}", tag=f"bank{2 + t % 2}")
            for c in range(S // P):
                cols = slice(P * c, P * (c + 1))
                nc.tensor.transpose(back[:, cols], gain_turned[t][:, cols], identity[:])
            nc.scalar.copy(ds_gain[t][:, S:], back[:])

        def put_ds(t):
            page[t] = sb([P, U], F32, f"page{t}")
            nc.vector.tensor_copy(page[t][:].indirect(n4_t[:]), ds_gain[t][:, :S])

        def put_up(t):
            nc.vector.tensor_tensor(page[t][:].indirect(n5_t[:]), h2[t][:], ds_gain[t][:, S:], ALU.add)
            nc.sync.dma_start(out_rows[t], page[t][:])

        for h in range(2):
            for t in range(2):
                second_product(t, h)
                put_h2(t, HALF * h, HALF * (h + 1))
        for t in range(2):
            negate(t)
        for t in range(2):
            make_gain(t)
            put_ds(t)
        for t in range(2, TILES):
            for h in range(2):
                second_product(t, h)
            negate(t)
            put_h2(t, 0, S)
            put_up(t - 2)
            make_gain(t)
        for t in range(2, TILES):
            put_ds(t)
        for t in range(2, TILES):
            put_up(t)
